import numpy as np
import ml_dtypes


def mxq(x, axis, fmt="e4m3"):
    dtype, down = {"e4m3": (ml_dtypes.float8_e4m3fn, 7), "e5m2": (ml_dtypes.float8_e5m2, 14)}[fmt]
    v = np.moveaxis(np.asarray(x, np.float32).astype(ml_dtypes.bfloat16).astype(np.float64), axis, -1)
    blocks = v.reshape(v.shape[:-1] + (-1, 32))
    amax = np.abs(blocks).max(-1, keepdims=True)
    byte = np.maximum(np.where(amax > 0, np.frexp(amax)[1] - 1 + 127, 0) - down, 1)
    scale = np.exp2(byte - 127.0)
    codes = (blocks / scale).astype(np.float32).astype(dtype).astype(np.float64)
    return np.moveaxis((codes * scale).reshape(v.shape), -1, axis)


WIDE = False


def mx_kscale(k):
    if not WIDE:
        return np.ones(k)
    levels = np.array([24, -24, 12, -12, 0])
    if k % 512:
        return np.exp2(np.random.permutation(np.resize(levels, k // 32))).repeat(32)
    a = np.empty((k // 512, 16))
    for p in range(k // 512):
        a[p, :8] = np.random.permutation(np.resize(levels, 8))
        for g in range(8):
            far = levels[np.abs(levels - a[p, g]) >= 10]
            a[p, g + 8] = far[np.random.randint(len(far))]
    return np.exp2(a.ravel()).repeat(32)


def f64(x):
    return np.asarray(x).astype(np.float64)


def striped(idx):
    return np.tile(idx.reshape(-1, 16).T, (8, 1)).astype(np.uint16)


def unstriped(offs):
    return offs[:16].T.reshape(-1).astype(np.int64)


E2M1 = np.array([0.0, 0.5, 1.0, 1.5, 2.0, 3.0, 4.0, 6.0, -0.0, -0.5, -1.0, -1.5, -2.0, -3.0, -4.0, -6.0])


def pack_weight(w, fmt):
    k, n = w.shape
    w = f64(np.asarray(w, np.float32).astype(ml_dtypes.bfloat16)).reshape(k // 32, 32, n)
    amax = np.abs(w).max(1)
    if fmt == "e4m3":
        byte = np.frexp(amax)[1] - 1 + 127 - 7
    else:
        mant, ex = np.frexp(amax / 6.0)
        byte = np.where(mant > 0.5, ex, ex - 1) + 127
    byte = np.clip(np.where(amax > 0, byte, 1), 1, 254)
    scaled = (w * np.exp2(127.0 - byte)[:, None, :]).reshape(k, n).astype(np.float32)
    by_word = np.ascontiguousarray(scaled.reshape(k // 512, 128, 4, n).transpose(0, 1, 3, 2))
    if fmt == "e4m3":
        words = by_word.astype(ml_dtypes.float8_e4m3fn).view(np.uint8)
    else:
        c = by_word.astype(ml_dtypes.float4_e2m1fn).view(np.uint8) & 0xF
        words = (c[..., 0::2] | (c[..., 1::2] << 4)).reshape(k // 512, 128, 2 * n)
    return np.ascontiguousarray(words), np.ascontiguousarray(byte.astype(np.uint8).reshape(k // 512, 16, n))


def unpack_weight(words, scales, fmt):
    g, _, n = scales.shape
    words = np.ascontiguousarray(words).reshape(g, 128, n, -1)
    if fmt == "e4m3":
        vals = words.view(ml_dtypes.float8_e4m3fn).astype(np.float64)
    else:
        nib = np.empty((g, 128, n, 4), np.uint8)
        nib[..., 0::2] = words & 0xF
        nib[..., 1::2] = words >> 4
        vals = E2M1[nib]
    vals = vals * np.repeat(np.exp2(scales.astype(np.float64) - 127.0), 8, axis=1)[..., None]
    return vals.transpose(0, 1, 3, 2).reshape(g * 512, n)


def planes(y):
    n, m = y.shape
    v = y.astype(np.float32).astype(ml_dtypes.bfloat16).astype(np.float64).reshape(n // 32, 32, m)
    top = np.abs(v).max(1)
    byte = np.clip(np.where(top > 0, np.frexp(top)[1] - 1 + 127 - 7, 1), 1, 254)
    codes = (v * np.exp2(127.0 - byte)[:, None, :]).reshape(n, m).astype(np.float32).astype(ml_dtypes.float8_e4m3fn).view(np.uint8)
    words = codes.reshape(n // 512, 128, 4, m).transpose(0, 1, 3, 2)
    return np.ascontiguousarray(words), np.ascontiguousarray(byte.astype(np.uint8).reshape(n // 512, 16, m))


K, N, T, J = 1024, 512, 4096, 1024


def setup_inputs():
    n = np.random.standard_normal
    s = mx_kscale(K)[:, None]
    wv = n((K, N)) / np.sqrt(K) / s
    p_tab = pack_weight(n((K, T)) * s, "e4m3")
    p_wk = pack_weight(n((K, N)) / np.sqrt(K) / s, "e2m1")
    p_wv4 = pack_weight(wv[512:], "e2m1")
    return {
        "tab_words": p_tab[0],
        "tab_scales": p_tab[1],
        "wk_words": p_wk[0],
        "wk_scales": p_wk[1],
        "wv8": (wv[:512]).astype(np.float32),
        "wv4_words": p_wv4[0],
        "wv4_scales": p_wv4[1],
        "st": (n((N, J))).astype(np.float32),
        "rT": (n((N, T))).astype(np.float32),
        "offs": striped(np.random.permutation(T)[:J]),
    }


def reference(tab_words, tab_scales, wk_words, wk_scales, wv8, wv4_words, wv4_scales, st, rT, offs):
    idx = unstriped(offs)
    tab_ = unpack_weight(tab_words, tab_scales, "e4m3")[:, idx]
    wk_ = unpack_weight(wk_words, wk_scales, "e2m1")
    wv8_ = mxq(f64(wv8), 0, "e4m3")
    wv4_ = unpack_weight(wv4_words, wv4_scales, "e2m1")
    ke = wk_.T @ tab_
    ve = wv8_.T @ tab_[:512] + wv4_.T @ tab_[512:]
    gate = np.tanh(ke * f64(st))
    out_0 = f64(rT)[:, idx] + gate * ve
    return (out_0,) + planes(out_0)

@@ -1,0 +1,195 @@
+from contextlib import ExitStack
+
+import concourse.mybir as mybir
+
+K, N, T, J = 1024, 512, 4096, 1024
+FLOPS = 2 * 2 * K * N * J
+
+F32 = mybir.dt.float32
+BF16 = mybir.dt.bfloat16
+I32 = mybir.dt.int32
+U32 = mybir.dt.uint32
+U16 = mybir.dt.uint16
+U8 = mybir.dt.uint8
+FP8X4 = mybir.dt.float8_e4m3fn_x4
+FP4X4 = mybir.dt.float4_e2m1fn_x4
+MULT = mybir.AluOpType.mult
+ADD = mybir.AluOpType.add
+TANH = mybir.ActivationFunctionType.Tanh
+
+P = 128
+PACK = 4
+PASSES = K // (P * PACK)
+BANK = 512
+HALVES = J // BANK
+CHUNK = 256
+CHUNKS = J // CHUNK
+QUADS = 4
+ROWS = 16
+
+
+def tile_list_engram_qf_tanhLP_kernel(
+    tc, tab_words, tab_scales, wk_words, wk_scales, wv8, wv4_words, wv4_scales, st, rT, offs, out_0, out_1, out_2
+):
+    nc = tc.nc
+    with ExitStack() as ctx:
+        keep = ctx.enter_context(tc.tile_pool(name="keep", bufs=1))
+        psum = ctx.enter_context(tc.psum_pool(name="psum", bufs=1))
+
+        def sb(name, shape, dtype):
+            return keep.tile(shape, dtype, name=name, align_bytes=64)
+
+        offsets = sb("offsets", [P, J // 16], U16)
+        tab_s = sb("tab_s", [P, T], U8)
+        tab_w = [sb("tab_w%d" % a, [P, T], U32) for a in range(PASSES)]
+        w4_raw = sb("w4_raw", [P, 3, 2 * N], U8)
+        s4_raw = sb("s4_raw", [P, 3, N], U8)
+        w4 = sb("w4", [P, 3, 2 * N], U8)
+        s4 = sb("s4", [P, 3, N], U8)
+        wv8_raw = sb("wv8_raw", [P, PACK, N], F32)
+        wv8_bf = sb("wv8_bf", [P, N * PACK], BF16)
+        wv8_w = sb("wv8_w", [P, N], U32)
+        wv8_s = sb("wv8_s", [P, N], U8)
+        st_sb = [sb("st%d" % t, [P, J], F32) for t in range(PACK)]
+        r_sb = [sb("r%d" % t, [P, T], F32) for t in range(PACK)]
+        got_s = sb("got_s", [P, J], U8)
+        got_w = [[sb("got_w%d_%d" % (a, h), [P, BANK], U32) for h in range(HALVES)] for a in range(PASSES)]
+        plane = [sb("plane%d" % a, [P, J], U8) for a in range(PASSES)]
+
+        nc.vector.memset(s4_raw[:].rearrange("p a n -> p (a n)").bitcast(I32), 0)
+        nc.vector.memset(tab_s[32:64, :].bitcast(I32), 0)
+        nc.vector.memset(tab_s[64:128, :].bitcast(I32), 0)
+        for a in range(PASSES):
+            nc.vector.memset(plane[a][:].bitcast(I32), 0)
+
+        st_rows = st.rearrange("(p t) j -> p t j", t=PACK)
+        r_rows = rT.rearrange("(p t) c -> p t c", t=PACK)
+        nc.sync.dma_start(offsets[:], offs)
+        nc.sync.dma_start(tab_s[0 : PASSES * ROWS, :].bitcast(I32), tab_scales.rearrange("a q c -> (a q) c").bitcast(I32))
+        nc.sync.dma_start(tab_w[0][:].bitcast(I32), tab_words[0].rearrange("p c i -> p (c i)").bitcast(I32))
+        nc.sync.dma_start(w4_raw[:, 0:2, :].bitcast(I32), wk_words.rearrange("a p b -> p a b").bitcast(I32))
+        nc.sync.dma_start(w4_raw[:, 2, :].bitcast(I32), wv4_words[0].bitcast(I32))
+        nc.sync.dma_start(tab_w[1][:].bitcast(I32), tab_words[1].rearrange("p c i -> p (c i)").bitcast(I32))
+        nc.sync.dma_start(wv8_raw[:], wv8.rearrange("(p i) n -> p i n", i=PACK))
+        for t in range(PACK):
+            nc.sync.dma_start(st_sb[t][:], st_rows[:, t, :])
+        for t in range(PACK):
+            nc.sync.dma_start(r_sb[t][:], r_rows[:, t, :])
+        for q in range(QUADS):
+            live = slice(32 * q, 32 * q + 4)
+            rows = slice(4 * q, 4 * q + 4)
+            nc.gpsimd.dma_start(s4_raw[live, 0:2, :].bitcast(I32), wk_scales[:, rows, :].rearrange("a r n -> r a n").bitcast(I32))
+            nc.gpsimd.dma_start(s4_raw[live, 2, :].bitcast(I32), wv4_scales[0, rows, :].bitcast(I32))
+
+        nc.vector.tensor_copy(got_s[:], tab_s[:].indirect(offsets[:]))
+        for a in range(PASSES):
+            for q in range(QUADS):
+                row = ROWS * a + 4 * q
+                nc.gpsimd.dma_start(plane[a][32 * q : 32 * q + 4, :].bitcast(I32), got_s[row : row + 4, :].bitcast(I32))
+
+        def listed(lo, count):
+            return offsets[:, lo // 16 : (lo + count) // 16]
+
+        def gather_words(a):
+            for h in range(HALVES):
+                nc.vector.tensor_copy(got_w[a][h][:], tab_w[a][:].indirect(listed(h * BANK, BANK)))
+
+        gather_words(0)
+        nc.vector.tensor_copy(
+            w4[:].bitcast(U16).rearrange("p a (t m) -> p a t m", t=PACK),
+            w4_raw[:].bitcast(U16).rearrange("p a (m t) -> p a t m", t=PACK),
+        )
+        nc.vector.tensor_copy(
+            s4[:].rearrange("p a (t m) -> p a t m", t=PACK),
+            s4_raw[:].rearrange("p a (m t) -> p a t m", t=PACK),
+        )
+        gather_words(1)
+
+        nc.scalar.copy(
+            wv8_bf[:].rearrange("p (t m i) -> p m t i", t=PACK, i=PACK),
+            wv8_raw[:].rearrange("p i (m t) -> p m t i", t=PACK),
+        )
+
+        def fp4(a, t):
+            return w4[:, a, 2 * P * t : 2 * P * (t + 1)].bitcast(FP4X4), s4[:, a, P * t : P * (t + 1)]
+
+        def product(bank, h, stationary):
+            for a in range(PASSES):
+                codes, scales = stationary[a]
+                nc.tensor.matmul_mx(
+                    out=bank[:],
+                    lhsT=codes,
+                    lhsT_scale=scales,
+                    rhs=got_w[a][h][:].bitcast(FP8X4),
+                    rhs_scale=plane[a][:, h * BANK : (h + 1) * BANK],
+                    start=(a == 0),
+                    stop=(a == PASSES - 1),
+                )
+
+        gate = [sb("gate%d" % t, [P, J], F32) for t in range(PACK)]
+        gated = [sb("gated%d" % t, [P, J], F32) for t in range(PACK)]
+
+        def key_stage(t):
+            for h in range(HALVES):
+                cols = slice(h * BANK, (h + 1) * BANK)
+                ke = psum.tile([P, BANK], F32, name="ke", tag="ke%d_%d" % (t % 2, h))
+                product(ke, h, [fp4(0, t), fp4(1, t)])
+                arg = keep.tile([P, BANK], F32, name="arg", tag="arg", bufs=4)
+                nc.vector.tensor_tensor(arg[:], ke[:], st_sb[t][:, cols], MULT)
+                nc.scalar.activation(gate[t][:, cols], arg[:], TANH)
+
+        def value_stage(t):
+            for h in range(HALVES):
+                cols = slice(h * BANK, (h + 1) * BANK)
+                ve = psum.tile([P, BANK], F32, name="ve", tag="ve%d_%d" % (t % 2, h))
+                e4 = (wv8_w[:, P * t : P * (t + 1)].bitcast(FP8X4), wv8_s[:, P * t : P * (t + 1)])
+                product(ve, h, [e4, fp4(2, t)])
+                nc.vector.tensor_tensor(gated[t][:, cols], ve[:], gate[t][:, cols], MULT)
+
+        key_stage(0)
+        key_stage(1)
+        nc.vector.quantize_mx(out=wv8_w[:].bitcast(FP8X4), scales=wv8_s[:], in_=wv8_bf[:])
+        key_stage(2)
+        value_stage(0)
+        key_stage(3)
+        for t in range(1, PACK):
+            value_stage(t)
+
+        out_rows = out_0.rearrange("(p t) j -> p t j", t=PACK)
+        out_words = out_1[0].rearrange("p j i -> p (j i)").bitcast(I32)
+        y_lo = sb("y_lo", [P, 2, J], F32)
+        y_hi = [sb("y_hi%d" % c, [P, 2, CHUNK], F32) for c in range(CHUNKS)]
+        y_bf = [sb("y_bf%d" % c, [P, CHUNK, PACK], BF16) for c in range(CHUNKS)]
+        y_w = [sb("y_w%d" % c, [P, CHUNK], U32) for c in range(CHUNKS)]
+        y_s = sb("y_s", [P, J], U8)
+
+        for t in range(2):
+            nc.vector.tensor_tensor(y_lo[:, t, :], r_sb[t][:].indirect(offsets[:]), gated[t][:], ADD)
+            nc.sync.dma_start(out_rows[:, t, :], y_lo[:, t, :])
+        for c in range(CHUNKS):
+            cols = slice(c * CHUNK, (c + 1) * CHUNK)
+            nc.scalar.copy(y_bf[c][:, :, 0:2], y_lo[:, :, cols].rearrange("p t j -> p j t"))
+
+        def add_record(t, c):
+            cols = slice(c * CHUNK, (c + 1) * CHUNK)
+            nc.vector.tensor_tensor(y_hi[c][:, t - 2, :], r_sb[t][:].indirect(listed(c * CHUNK, CHUNK)), gated[t][:, cols], ADD)
+
+        def finish(c):
+            cols = slice(c * CHUNK, (c + 1) * CHUNK)
+            nc.vector.quantize_mx(
+                out=y_w[c][:].bitcast(FP8X4), scales=y_s[:, cols], in_=y_bf[c][:].rearrange("p j t -> p (j t)")
+            )
+            nc.sync.dma_start(out_words[:, cols], y_w[c][:].bitcast(I32))
+
+        for c in range(CHUNKS):
+            add_record(2, c)
+        for c in range(CHUNKS):
+            cols = slice(c * CHUNK, (c + 1) * CHUNK)
+            add_record(3, c)
+            nc.sync.dma_start(out_rows[:, 2:4, cols], y_hi[c][:])
+            nc.scalar.copy(y_bf[c][:, :, 2:4], y_hi[c][:].rearrange("p t j -> p j t"))
+            if c > 0:
+                finish(c - 1)
+        finish(CHUNKS - 1)
+        for q in range(QUADS):
+            nc.scalar.dma_start(out_2[0, 4 * q : 4 * q + 4, :].bitcast(I32), y_s[32 * q : 32 * q + 4, :].bitcast(I32))

@@ -64,28 +64,43 @@ def tile_list_engram_qf_tanhLP_kernel(
 
         st_rows = st.rearrange("(p t) j -> p t j", t=PACK)
         r_rows = rT.rearrange("(p t) c -> p t c", t=PACK)
+        def load_words(a, half):
+            cols = slice(half * T // 2, (half + 1) * T // 2)
+            nc.sync.dma_start(
+                tab_w[a][:, cols].bitcast(I32), tab_words[a].rearrange("p c i -> p (c i)").bitcast(I32)[:, cols]
+            )
+
+        def load_weight_scales(q):
+            live = slice(32 * q, 32 * q + 4)
+            rows = slice(4 * q, 4 * q + 4)
+            nc.sync.dma_start(s4_raw[live, 0:2, :].bitcast(I32), wk_scales[:, rows, :].rearrange("a r n -> r a n").bitcast(I32))
+            nc.sync.dma_start(s4_raw[live, 2, :].bitcast(I32), wv4_scales[0, rows, :].bitcast(I32))
+
+        def move_scales(a):
+            for q in range(QUADS):
+                row = ROWS * a + 4 * q
+                nc.sync.dma_start(plane[a][32 * q : 32 * q + 4, :].bitcast(I32), got_s[row : row + 4, :].bitcast(I32))
+
         nc.sync.dma_start(offsets[:], offs)
         nc.sync.dma_start(tab_s[0 : PASSES * ROWS, :].bitcast(I32), tab_scales.rearrange("a q c -> (a q) c").bitcast(I32))
-        nc.sync.dma_start(tab_w[0][:].bitcast(I32), tab_words[0].rearrange("p c i -> p (c i)").bitcast(I32))
+        load_words(0, 0)
+        load_weight_scales(0)
+        load_words(0, 1)
+        load_weight_scales(1)
         nc.sync.dma_start(w4_raw[:, 0:2, :].bitcast(I32), wk_words.rearrange("a p b -> p a b").bitcast(I32))
+        load_weight_scales(2)
+        load_words(1, 0)
+        load_weight_scales(3)
         nc.sync.dma_start(w4_raw[:, 2, :].bitcast(I32), wv4_words[0].bitcast(I32))
-        nc.sync.dma_start(tab_w[1][:].bitcast(I32), tab_words[1].rearrange("p c i -> p (c i)").bitcast(I32))
+        load_words(1, 1)
+        nc.vector.tensor_copy(got_s[:], tab_s[:].indirect(offsets[:]))
+        move_scales(0)
         nc.sync.dma_start(wv8_raw[:], wv8.rearrange("(p i) n -> p i n", i=PACK))
+        move_scales(1)
         for t in range(PACK):
             nc.sync.dma_start(st_sb[t][:], st_rows[:, t, :])
         for t in range(PACK):
             nc.sync.dma_start(r_sb[t][:], r_rows[:, t, :])
-        for q in range(QUADS):
-            live = slice(32 * q, 32 * q + 4)
-            rows = slice(4 * q, 4 * q + 4)
-            nc.gpsimd.dma_start(s4_raw[live, 0:2, :].bitcast(I32), wk_scales[:, rows, :].rearrange("a r n -> r a n").bitcast(I32))
-            nc.gpsimd.dma_start(s4_raw[live, 2, :].bitcast(I32), wv4_scales[0, rows, :].bitcast(I32))
-
-        nc.vector.tensor_copy(got_s[:], tab_s[:].indirect(offsets[:]))
-        for a in range(PASSES):
-            for q in range(QUADS):
-                row = ROWS * a + 4 * q
-                nc.gpsimd.dma_start(plane[a][32 * q : 32 * q + 4, :].bitcast(I32), got_s[row : row + 4, :].bitcast(I32))
 
         def listed(lo, count):
             return offsets[:, lo // 16 : (lo + count) // 16]

@@ -42,63 +42,67 @@ def tile_list_engram_qf_tanhLP_kernel(
         offsets = sb("offsets", [P, J // 16], U16)
         tab_s = sb("tab_s", [P, T], U8)
         tab_w = [sb("tab_w%d" % a, [P, T], U32) for a in range(PASSES)]
-        w4_raw = sb("w4_raw", [P, 3, 2 * N], U8)
-        s4_raw = sb("s4_raw", [P, 3, N], U8)
-        w4 = sb("w4", [P, 3, 2 * N], U8)
-        s4 = sb("s4", [P, 3, N], U8)
+        wk_raw = sb("wk_raw", [P, PASSES, 2 * N], U8)
+        wk_s_raw = sb("wk_s_raw", [P, PASSES, N], U8)
+        wk_w = sb("wk_w", [P, PASSES, 2 * N], U8)
+        wk_s = sb("wk_s", [P, PASSES, N], U8)
+        wv4_raw = sb("wv4_raw", [P, 1, 2 * N], U8)
+        wv4_s_raw = sb("wv4_s_raw", [P, 1, N], U8)
+        wv4_w = sb("wv4_w", [P, 1, 2 * N], U8)
+        wv4_s = sb("wv4_s", [P, 1, N], U8)
         wv8_raw = sb("wv8_raw", [P, PACK, N], F32)
         wv8_bf = sb("wv8_bf", [P, N * PACK], BF16)
         wv8_w = sb("wv8_w", [P, N], U32)
         wv8_s = sb("wv8_s", [P, N], U8)
-        st_sb = [sb("st%d" % t, [P, J], F32) for t in range(PACK)]
+        st_sb = [sb("st%d" % u, [P, 2, J], F32) for u in range(2)]
         r_sb = [sb("r%d" % t, [P, T], F32) for t in range(PACK)]
         got_s = sb("got_s", [P, J], U8)
         got_w = [[sb("got_w%d_%d" % (a, h), [P, BANK], U32) for h in range(HALVES)] for a in range(PASSES)]
         plane = [sb("plane%d" % a, [P, J], U8) for a in range(PASSES)]
 
-        nc.vector.memset(s4_raw[:].rearrange("p a n -> p (a n)").bitcast(I32), 0)
-        nc.vector.memset(tab_s[32:64, :].bitcast(I32), 0)
-        nc.vector.memset(tab_s[64:128, :].bitcast(I32), 0)
+        first_row = P - PASSES * ROWS
+        nc.gpsimd.memset(wk_s_raw[:].rearrange("p a n -> p (a n)").bitcast(I32), 0)
+        nc.gpsimd.memset(wv4_s_raw[:, 0, :].bitcast(I32), 0)
+        nc.vector.memset(tab_s[0:first_row, :].bitcast(I32), 0)
         for a in range(PASSES):
             nc.vector.memset(plane[a][:].bitcast(I32), 0)
 
         st_rows = st.rearrange("(p t) j -> p t j", t=PACK)
         r_rows = rT.rearrange("(p t) c -> p t c", t=PACK)
-        def load_words(a, half):
-            cols = slice(half * T // 2, (half + 1) * T // 2)
+
+        def load_words(a, cols):
             nc.sync.dma_start(
                 tab_w[a][:, cols].bitcast(I32), tab_words[a].rearrange("p c i -> p (c i)").bitcast(I32)[:, cols]
             )
 
-        def load_weight_scales(q):
-            live = slice(32 * q, 32 * q + 4)
-            rows = slice(4 * q, 4 * q + 4)
-            nc.sync.dma_start(s4_raw[live, 0:2, :].bitcast(I32), wk_scales[:, rows, :].rearrange("a r n -> r a n").bitcast(I32))
-            nc.sync.dma_start(s4_raw[live, 2, :].bitcast(I32), wv4_scales[0, rows, :].bitcast(I32))
-
-        def move_scales(a):
+        def load_weight_scales(tile, scales):
             for q in range(QUADS):
-                row = ROWS * a + 4 * q
+                nc.gpsimd.dma_start(
+                    tile[32 * q : 32 * q + 4, :, :].bitcast(I32),
+                    scales[:, 4 * q : 4 * q + 4, :].rearrange("a r n -> r a n").bitcast(I32),
+                )
+
+        def move_scales(blocks):
+            for a, q in blocks:
+                row = first_row + ROWS * a + 4 * q
                 nc.sync.dma_start(plane[a][32 * q : 32 * q + 4, :].bitcast(I32), got_s[row : row + 4, :].bitcast(I32))
 
+        blocks = [(a, q) for a in range(PASSES) for q in range(QUADS)]
         nc.sync.dma_start(offsets[:], offs)
-        nc.sync.dma_start(tab_s[0 : PASSES * ROWS, :].bitcast(I32), tab_scales.rearrange("a q c -> (a q) c").bitcast(I32))
-        load_words(0, 0)
-        load_weight_scales(0)
-        load_words(0, 1)
-        load_weight_scales(1)
-        nc.sync.dma_start(w4_raw[:, 0:2, :].bitcast(I32), wk_words.rearrange("a p b -> p a b").bitcast(I32))
-        load_weight_scales(2)
-        load_words(1, 0)
-        load_weight_scales(3)
-        nc.sync.dma_start(w4_raw[:, 2, :].bitcast(I32), wv4_words[0].bitcast(I32))
-        load_words(1, 1)
+        nc.sync.dma_start(tab_s[first_row:P, :].bitcast(I32), tab_scales.rearrange("a q c -> (a q) c").bitcast(I32))
+        load_weight_scales(wk_s_raw, wk_scales)
+        load_weight_scales(wv4_s_raw, wv4_scales)
+        load_words(0, slice(0, T))
+        nc.sync.dma_start(wk_raw[:].bitcast(I32), wk_words.rearrange("a p b -> p a b").bitcast(I32))
+        load_words(1, slice(0, T // 2))
+        nc.sync.dma_start(wv4_raw[:].bitcast(I32), wv4_words.rearrange("a p b -> p a b").bitcast(I32))
         nc.vector.tensor_copy(got_s[:], tab_s[:].indirect(offsets[:]))
-        move_scales(0)
+        move_scales(blocks[:5])
+        load_words(1, slice(T // 2, T))
+        move_scales(blocks[5:])
         nc.sync.dma_start(wv8_raw[:], wv8.rearrange("(p i) n -> p i n", i=PACK))
-        move_scales(1)
-        for t in range(PACK):
-            nc.sync.dma_start(st_sb[t][:], st_rows[:, t, :])
+        nc.sync.dma_start(st_sb[0][:], st_rows[:, 0:2, :])
+        nc.sync.dma_start(st_sb[1][:], st_rows[:, 2:4, :])
         for t in range(PACK):
             nc.sync.dma_start(r_sb[t][:], r_rows[:, t, :])
 
@@ -109,15 +113,19 @@ def tile_list_engram_qf_tanhLP_kernel(
             for h in range(HALVES):
                 nc.vector.tensor_copy(got_w[a][h][:], tab_w[a][:].indirect(listed(h * BANK, BANK)))
 
+        def deal(words, scales, words_raw, scales_raw):
+            nc.vector.tensor_copy(
+                words[:].bitcast(U16).rearrange("p a (t m) -> p a t m", t=PACK),
+                words_raw[:].bitcast(U16).rearrange("p a (m t) -> p a t m", t=PACK),
+            )
+            nc.vector.tensor_copy(
+                scales[:].rearrange("p a (t m) -> p a t m", t=PACK),
+                scales_raw[:].rearrange("p a (m t) -> p a t m", t=PACK),
+            )
+
         gather_words(0)
-        nc.vector.tensor_copy(
-            w4[:].bitcast(U16).rearrange("p a (t m) -> p a t m", t=PACK),
-            w4_raw[:].bitcast(U16).rearrange("p a (m t) -> p a t m", t=PACK),
-        )
-        nc.vector.tensor_copy(
-            s4[:].rearrange("p a (t m) -> p a t m", t=PACK),
-            s4_raw[:].rearrange("p a (m t) -> p a t m", t=PACK),
-        )
+        deal(wk_w, wk_s, wk_raw, wk_s_raw)
+        deal(wv4_w, wv4_s, wv4_raw, wv4_s_raw)
         gather_words(1)
 
         nc.scalar.copy(
@@ -125,8 +133,8 @@ def tile_list_engram_qf_tanhLP_kernel(
             wv8_raw[:].rearrange("p i (m t) -> p m t i", t=PACK),
         )
 
-        def fp4(a, t):
-            return w4[:, a, 2 * P * t : 2 * P * (t + 1)].bitcast(FP4X4), s4[:, a, P * t : P * (t + 1)]
+        def fp4(words, scales, a, t):
+            return words[:, a, 2 * P * t : 2 * P * (t + 1)].bitcast(FP4X4), scales[:, a, P * t : P * (t + 1)]
 
         def product(bank, h, stationary):
             for a in range(PASSES):
@@ -148,63 +156,60 @@ def tile_list_engram_qf_tanhLP_kernel(
             for h in range(HALVES):
                 cols = slice(h * BANK, (h + 1) * BANK)
                 ke = psum.tile([P, BANK], F32, name="ke", tag="ke%d_%d" % (t % 2, h))
-                product(ke, h, [fp4(0, t), fp4(1, t)])
-                arg = keep.tile([P, BANK], F32, name="arg", tag="arg", bufs=4)
-                nc.vector.tensor_tensor(arg[:], ke[:], st_sb[t][:, cols], MULT)
-                nc.scalar.activation(gate[t][:, cols], arg[:], TANH)
+                product(ke, h, [fp4(wk_w, wk_s, 0, t), fp4(wk_w, wk_s, 1, t)])
+                nc.vector.tensor_tensor(gate[t][:, cols], ke[:], st_sb[t // 2][:, t % 2, cols], MULT)
+                nc.scalar.activation(gate[t][:, cols], gate[t][:, cols], TANH)
 
         def value_stage(t):
             for h in range(HALVES):
                 cols = slice(h * BANK, (h + 1) * BANK)
                 ve = psum.tile([P, BANK], F32, name="ve", tag="ve%d_%d" % (t % 2, h))
                 e4 = (wv8_w[:, P * t : P * (t + 1)].bitcast(FP8X4), wv8_s[:, P * t : P * (t + 1)])
-                product(ve, h, [e4, fp4(2, t)])
+                product(ve, h, [e4, fp4(wv4_w, wv4_s, 0, t)])
                 nc.vector.tensor_tensor(gated[t][:, cols], ve[:], gate[t][:, cols], MULT)
 
         key_stage(0)
-        key_stage(1)
         nc.vector.quantize_mx(out=wv8_w[:].bitcast(FP8X4), scales=wv8_s[:], in_=wv8_bf[:])
-        key_stage(2)
-        value_stage(0)
-        key_stage(3)
         for t in range(1, PACK):
+            key_stage(t)
+        for t in range(PACK):
             value_stage(t)
 
         out_rows = out_0.rearrange("(p t) j -> p t j", t=PACK)
         out_words = out_1[0].rearrange("p j i -> p (j i)").bitcast(I32)
         y_lo = sb("y_lo", [P, 2, J], F32)
-        y_hi = [sb("y_hi%d" % c, [P, 2, CHUNK], F32) for c in range(CHUNKS)]
-        y_bf = [sb("y_bf%d" % c, [P, CHUNK, PACK], BF16) for c in range(CHUNKS)]
-        y_w = [sb("y_w%d" % c, [P, CHUNK], U32) for c in range(CHUNKS)]
+        y_hi = sb("y_hi", [P, 2, J], F32)
+        y_bf = sb("y_bf", [P, J * PACK], BF16)
+        y_w = sb("y_w", [P, J], U32)
         y_s = sb("y_s", [P, J], U8)
+        y_by_column = y_bf[:].rearrange("p (j t) -> p j t", t=PACK)
 
         for t in range(2):
             nc.vector.tensor_tensor(y_lo[:, t, :], r_sb[t][:].indirect(offsets[:]), gated[t][:], ADD)
-            nc.sync.dma_start(out_rows[:, t, :], y_lo[:, t, :])
-        for c in range(CHUNKS):
-            cols = slice(c * CHUNK, (c + 1) * CHUNK)
-            nc.scalar.copy(y_bf[c][:, :, 0:2], y_lo[:, :, cols].rearrange("p t j -> p j t"))
+        nc.sync.dma_start(out_rows[:, 0:2, :], y_lo[:])
+        nc.scalar.copy(y_by_column[:, :, 0:2], y_lo[:].rearrange("p t j -> p j t"))
+        nc.vector.tensor_tensor(y_hi[:, 0, :], r_sb[2][:].indirect(offsets[:]), gated[2][:], ADD)
+        nc.sync.dma_start(out_rows[:, 2, :], y_hi[:, 0, :])
 
-        def add_record(t, c):
-            cols = slice(c * CHUNK, (c + 1) * CHUNK)
-            nc.vector.tensor_tensor(y_hi[c][:, t - 2, :], r_sb[t][:].indirect(listed(c * CHUNK, CHUNK)), gated[t][:, cols], ADD)
+        def add_record(lo, hi):
+            nc.vector.tensor_tensor(y_hi[:, 1, lo:hi], r_sb[3][:].indirect(listed(lo, hi - lo)), gated[3][:, lo:hi], ADD)
+            nc.scalar.copy(y_by_column[:, lo:hi, 2:4], y_hi[:, :, lo:hi].rearrange("p t j -> p j t"))
 
-        def finish(c):
-            cols = slice(c * CHUNK, (c + 1) * CHUNK)
+        def quantise(lo, hi):
             nc.vector.quantize_mx(
-                out=y_w[c][:].bitcast(FP8X4), scales=y_s[:, cols], in_=y_bf[c][:].rearrange("p j t -> p (j t)")
+                out=y_w[:, lo:hi].bitcast(FP8X4), scales=y_s[:, lo:hi], in_=y_bf[:, PACK * lo : PACK * hi]
             )
-            nc.sync.dma_start(out_words[:, cols], y_w[c][:].bitcast(I32))
 
-        for c in range(CHUNKS):
-            add_record(2, c)
-        for c in range(CHUNKS):
-            cols = slice(c * CHUNK, (c + 1) * CHUNK)
-            add_record(3, c)
-            nc.sync.dma_start(out_rows[:, 2:4, cols], y_hi[c][:])
-            nc.scalar.copy(y_bf[c][:, :, 2:4], y_hi[c][:].rearrange("p t j -> p j t"))
-            if c > 0:
-                finish(c - 1)
-        finish(CHUNKS - 1)
+        add_record(0, 128)
+        add_record(128, 512)
+        nc.sync.dma_start(out_rows[:, 3, 0:512], y_hi[:, 1, 0:512])
+        add_record(512, 768)
+        add_record(768, 1024)
+        nc.sync.dma_start(out_rows[:, 3, 512:1024], y_hi[:, 1, 512:1024])
+        quantise(0, 512)
+        nc.sync.dma_start(out_words[:, 0:512], y_w[:, 0:512].bitcast(I32))
+        quantise(512, 768)
+        quantise(768, 1024)
+        nc.sync.dma_start(out_words[:, 512:1024], y_w[:, 512:1024].bitcast(I32))
         for q in range(QUADS):
             nc.scalar.dma_start(out_2[0, 4 * q : 4 * q + 4, :].bitcast(I32), y_s[32 * q : 32 * q + 4, :].bitcast(I32))

from contextlib import ExitStack

import concourse.mybir as mybir

K, N, T, J = 1024, 512, 4096, 1024
FLOPS = 2 * 2 * K * N * J

F32 = mybir.dt.float32
BF16 = mybir.dt.bfloat16
I32 = mybir.dt.int32
U32 = mybir.dt.uint32
U16 = mybir.dt.uint16
U8 = mybir.dt.uint8
FP8X4 = mybir.dt.float8_e4m3fn_x4
FP4X4 = mybir.dt.float4_e2m1fn_x4
MULT = mybir.AluOpType.mult
ADD = mybir.AluOpType.add
TANH = mybir.ActivationFunctionType.Tanh

P = 128
PACK = 4
PASSES = K // (P * PACK)
BANK = 512
HALVES = J // BANK
CHUNK = 256
CHUNKS = J // CHUNK
QUADS = 4
ROWS = 16


def tile_list_engram_qf_tanhLP_kernel(
    tc, tab_words, tab_scales, wk_words, wk_scales, wv8, wv4_words, wv4_scales, st, rT, offs, out_0, out_1, out_2
):
    nc = tc.nc
    with ExitStack() as ctx:
        keep = ctx.enter_context(tc.tile_pool(name="keep", bufs=1))
        psum = ctx.enter_context(tc.psum_pool(name="psum", bufs=1))

        def sb(name, shape, dtype):
            return keep.tile(shape, dtype, name=name, align_bytes=64)

        offsets = sb("offsets", [P, J // 16], U16)
        tab_s = sb("tab_s", [P, T], U8)
        tab_w = [sb("tab_w%d" % a, [P, T], U32) for a in range(PASSES)]
        wk_raw = sb("wk_raw", [P, PASSES, 2 * N], U8)
        wk_s_raw = sb("wk_s_raw", [P, PASSES, N], U8)
        wk_w = sb("wk_w", [P, PASSES, 2 * N], U8)
        wk_s = sb("wk_s", [P, PASSES, N], U8)
        wv4_raw = sb("wv4_raw", [P, 1, 2 * N], U8)
        wv4_s_raw = sb("wv4_s_raw", [P, 1, N], U8)
        wv4_w = sb("wv4_w", [P, 1, 2 * N], U8)
        wv4_s = sb("wv4_s", [P, 1, N], U8)
        wv8_raw = sb("wv8_raw", [P, PACK, N], F32)
        wv8_bf = sb("wv8_bf", [P, N * PACK], BF16)
        wv8_w = sb("wv8_w", [P, N], U32)
        wv8_s = sb("wv8_s", [P, N], U8)
        st_sb = [sb("st%d" % u, [P, 2, J], F32) for u in range(2)]
        r_sb = [sb("r%d" % t, [P, T], F32) for t in range(PACK)]
        got_s = sb("got_s", [P, J], U8)
        got_w = [[sb("got_w%d_%d" % (a, h), [P, BANK], U32) for h in range(HALVES)] for a in range(PASSES)]
        plane = [sb("plane%d" % a, [P, J], U8) for a in range(PASSES)]

        first_row = P - PASSES * ROWS
        nc.gpsimd.memset(wk_s_raw[:].rearrange("p a n -> p (a n)").bitcast(I32), 0)
        nc.gpsimd.memset(wv4_s_raw[:, 0, :].bitcast(I32), 0)
        nc.vector.memset(tab_s[0:first_row, :].bitcast(I32), 0)
        for a in range(PASSES):
            nc.vector.memset(plane[a][:].bitcast(I32), 0)

        st_rows = st.rearrange("(p t) j -> p t j", t=PACK)
        r_rows = rT.rearrange("(p t) c -> p t c", t=PACK)

        def load_words(a, cols):
            nc.sync.dma_start(
                tab_w[a][:, cols].bitcast(I32), tab_words[a].rearrange("p c i -> p (c i)").bitcast(I32)[:, cols]
            )

        def load_weight_scales(tile, scales):
            for q in range(QUADS):
                nc.gpsimd.dma_start(
                    tile[32 * q : 32 * q + 4, :, :].bitcast(I32),
                    scales[:, 4 * q : 4 * q + 4, :].rearrange("a r n -> r a n").bitcast(I32),
                )

        def move_scales(blocks):
            for a, q in blocks:
                row = first_row + ROWS * a + 4 * q
                nc.sync.dma_start(plane[a][32 * q : 32 * q + 4, :].bitcast(I32), got_s[row : row + 4, :].bitcast(I32))

        blocks = [(a, q) for a in range(PASSES) for q in range(QUADS)]
        nc.sync.dma_start(offsets[:], offs)
        nc.sync.dma_start(tab_s[first_row:P, :].bitcast(I32), tab_scales.rearrange("a q c -> (a q) c").bitcast(I32))
        load_weight_scales(wk_s_raw, wk_scales)
        load_weight_scales(wv4_s_raw, wv4_scales)
        load_words(0, slice(0, T))
        nc.sync.dma_start(wk_raw[:].bitcast(I32), wk_words.rearrange("a p b -> p a b").bitcast(I32))
        load_words(1, slice(0, T // 2))
        nc.sync.dma_start(wv4_raw[:].bitcast(I32), wv4_words.rearrange("a p b -> p a b").bitcast(I32))
        nc.vector.tensor_copy(got_s[:], tab_s[:].indirect(offsets[:]))
        move_scales(blocks[:5])
        load_words(1, slice(T // 2, T))
        move_scales(blocks[5:])
        nc.sync.dma_start(wv8_raw[:], wv8.rearrange("(p i) n -> p i n", i=PACK))
        nc.sync.dma_start(st_sb[0][:], st_rows[:, 0:2, :])
        nc.sync.dma_start(st_sb[1][:], st_rows[:, 2:4, :])
        for t in range(PACK):
            nc.sync.dma_start(r_sb[t][:], r_rows[:, t, :])

        def listed(lo, count):
            return offsets[:, lo // 16 : (lo + count) // 16]

        def gather_words(a):
            for h in range(HALVES):
                nc.vector.tensor_copy(got_w[a][h][:], tab_w[a][:].indirect(listed(h * BANK, BANK)))

        def deal(words, scales, words_raw, scales_raw):
            nc.vector.tensor_copy(
                words[:].bitcast(U16).rearrange("p a (t m) -> p a t m", t=PACK),
                words_raw[:].bitcast(U16).rearrange("p a (m t) -> p a t m", t=PACK),
            )
            nc.vector.tensor_copy(
                scales[:].rearrange("p a (t m) -> p a t m", t=PACK),
                scales_raw[:].rearrange("p a (m t) -> p a t m", t=PACK),
            )

        gather_words(0)
        deal(wk_w, wk_s, wk_raw, wk_s_raw)
        deal(wv4_w, wv4_s, wv4_raw, wv4_s_raw)
        gather_words(1)

        nc.scalar.copy(
            wv8_bf[:].rearrange("p (t m i) -> p m t i", t=PACK, i=PACK),
            wv8_raw[:].rearrange("p i (m t) -> p m t i", t=PACK),
        )

        def fp4(words, scales, a, t):
            return words[:, a, 2 * P * t : 2 * P * (t + 1)].bitcast(FP4X4), scales[:, a, P * t : P * (t + 1)]

        def product(bank, h, stationary):
            for a in range(PASSES):
                codes, scales = stationary[a]
                nc.tensor.matmul_mx(
                    out=bank[:],
                    lhsT=codes,
                    lhsT_scale=scales,
                    rhs=got_w[a][h][:].bitcast(FP8X4),
                    rhs_scale=plane[a][:, h * BANK : (h + 1) * BANK],
                    start=(a == 0),
                    stop=(a == PASSES - 1),
                )

        gate = [sb("gate%d" % t, [P, J], F32) for t in range(PACK)]
        gated = [sb("gated%d" % t, [P, J], F32) for t in range(PACK)]

        def key_stage(t):
            for h in range(HALVES):
                cols = slice(h * BANK, (h + 1) * BANK)
                ke = psum.tile([P, BANK], F32, name="ke", tag="ke%d_%d" % (t % 2, h))
                product(ke, h, [fp4(wk_w, wk_s, 0, t), fp4(wk_w, wk_s, 1, t)])
                nc.vector.tensor_tensor(gate[t][:, cols], ke[:], st_sb[t // 2][:, t % 2, cols], MULT)
                nc.scalar.activation(gate[t][:, cols], gate[t][:, cols], TANH)

        def value_stage(t):
            for h in range(HALVES):
                cols = slice(h * BANK, (h + 1) * BANK)
                ve = psum.tile([P, BANK], F32, name="ve", tag="ve%d_%d" % (t % 2, h))
                e4 = (wv8_w[:, P * t : P * (t + 1)].bitcast(FP8X4), wv8_s[:, P * t : P * (t + 1)])
                product(ve, h, [e4, fp4(wv4_w, wv4_s, 0, t)])
                nc.vector.tensor_tensor(gated[t][:, cols], ve[:], gate[t][:, cols], MULT)

        key_stage(0)
        nc.vector.quantize_mx(out=wv8_w[:].bitcast(FP8X4), scales=wv8_s[:], in_=wv8_bf[:])
        for t in range(1, PACK):
            key_stage(t)
        for t in range(PACK):
            value_stage(t)

        out_rows = out_0.rearrange("(p t) j -> p t j", t=PACK)
        out_words = out_1[0].rearrange("p j i -> p (j i)").bitcast(I32)
        y_lo = sb("y_lo", [P, 2, J], F32)
        y_hi = sb("y_hi", [P, 2, J], F32)
        y_bf = sb("y_bf", [P, J * PACK], BF16)
        y_w = sb("y_w", [P, J], U32)
        y_s = sb("y_s", [P, J], U8)
        y_by_column = y_bf[:].rearrange("p (j t) -> p j t", t=PACK)

        for t in range(2):
            nc.vector.tensor_tensor(y_lo[:, t, :], r_sb[t][:].indirect(offsets[:]), gated[t][:], ADD)
        nc.sync.dma_start(out_rows[:, 0:2, :], y_lo[:])
        nc.scalar.copy(y_by_column[:, :, 0:2], y_lo[:].rearrange("p t j -> p j t"))
        nc.vector.tensor_tensor(y_hi[:, 0, :], r_sb[2][:].indirect(offsets[:]), gated[2][:], ADD)
        nc.sync.dma_start(out_rows[:, 2, :], y_hi[:, 0, :])

        def add_record(lo, hi):
            nc.vector.tensor_tensor(y_hi[:, 1, lo:hi], r_sb[3][:].indirect(listed(lo, hi - lo)), gated[3][:, lo:hi], ADD)
            nc.scalar.copy(y_by_column[:, lo:hi, 2:4], y_hi[:, :, lo:hi].rearrange("p t j -> p j t"))

        def quantise(lo, hi):
            nc.vector.quantize_mx(
                out=y_w[:, lo:hi].bitcast(FP8X4), scales=y_s[:, lo:hi], in_=y_bf[:, PACK * lo : PACK * hi]
            )

        add_record(0, 128)
        add_record(128, 512)
        nc.sync.dma_start(out_rows[:, 3, 0:512], y_hi[:, 1, 0:512])
        add_record(512, 768)
        add_record(768, 1024)
        nc.sync.dma_start(out_rows[:, 3, 512:1024], y_hi[:, 1, 512:1024])
        quantise(0, 512)
        nc.sync.dma_start(out_words[:, 0:512], y_w[:, 0:512].bitcast(I32))
        quantise(512, 768)
        quantise(768, 1024)
        nc.sync.dma_start(out_words[:, 512:1024], y_w[:, 512:1024].bitcast(I32))
        for q in range(QUADS):
            nc.scalar.dma_start(out_2[0, 4 * q : 4 * q + 4, :].bitcast(I32), y_s[32 * q : 32 * q + 4, :].bitcast(I32))
